import numpy as np
import ml_dtypes


def mxq(x, axis, fmt="e4m3"):
    dtype, down = {"e4m3": (ml_dtypes.float8_e4m3fn, 7), "e5m2": (ml_dtypes.float8_e5m2, 14)}[fmt]
    v = np.moveaxis(np.asarray(x, np.float32).astype(ml_dtypes.bfloat16).astype(np.float64), axis, -1)
    blocks = v.reshape(v.shape[:-1] + (-1, 32))
    amax = np.abs(blocks).max(-1, keepdims=True)
    byte = np.maximum(np.where(amax > 0, np.frexp(amax)[1] - 1 + 127, 0) - down, 1)
    scale = np.exp2(byte - 127.0)
    codes = (blocks / scale).astype(np.float32).astype(dtype).astype(np.float64)
    return np.moveaxis((codes * scale).reshape(v.shape), -1, axis)


WIDE = False


def mx_kscale(k):
    if not WIDE:
        return np.ones(k)
    levels = np.array([10, -10, 5, -5, 0])
    if k % 512:
        return np.exp2(np.random.permutation(np.resize(levels, k // 32))).repeat(32)
    a = np.empty((k // 512, 16))
    for p in range(k // 512):
        a[p, :8] = np.random.permutation(np.resize(levels, 8))
        for g in range(8):
            far = levels[np.abs(levels - a[p, g]) >= 10]
            a[p, g + 8] = far[np.random.randint(len(far))]
    return np.exp2(a.ravel()).repeat(32)


BF16 = ml_dtypes.bfloat16


def bf(x):
    return np.asarray(x, np.float32).astype(BF16)


def f64(x):
    return np.asarray(x).astype(np.float64)


E2M1 = np.array([0.0, 0.5, 1.0, 1.5, 2.0, 3.0, 4.0, 6.0, -0.0, -0.5, -1.0, -1.5, -2.0, -3.0, -4.0, -6.0])


def pack_weight(w, fmt):
    k, n = w.shape
    w = f64(bf(w)).reshape(k // 32, 32, n)
    amax = np.abs(w).max(1)
    if fmt == "e4m3":
        byte = np.frexp(amax)[1] - 1 + 127 - 7
    else:
        mant, ex = np.frexp(amax / 6.0)
        byte = np.where(mant > 0.5, ex, ex - 1) + 127
    byte = np.clip(np.where(amax > 0, byte, 1), 1, 254)
    scaled = (w * np.exp2(127.0 - byte)[:, None, :]).reshape(k, n).astype(np.float32)
    by_word = np.ascontiguousarray(scaled.reshape(k // 512, 128, 4, n).transpose(0, 1, 3, 2))
    if fmt == "e4m3":
        words = by_word.astype(ml_dtypes.float8_e4m3fn).view(np.uint8)
    else:
        c = by_word.astype(ml_dtypes.float4_e2m1fn).view(np.uint8) & 0xF
        words = c[..., 0::2] | (c[..., 1::2] << 4)
    return np.ascontiguousarray(words), np.ascontiguousarray(byte.astype(np.uint8).reshape(k // 512, 16, n))


def unpack_weight(words, scales, fmt):
    g, p, n, _ = words.shape
    if fmt == "e4m3":
        vals = np.ascontiguousarray(words).view(ml_dtypes.float8_e4m3fn).astype(np.float64)
    else:
        nib = np.empty((g, p, n, 4), np.uint8)
        nib[..., 0::2] = words & 0xF
        nib[..., 1::2] = words >> 4
        vals = E2M1[nib]
    vals = vals * np.repeat(np.exp2(scales.astype(np.float64) - 127.0), 8, axis=1)[..., None]
    return vals.transpose(0, 1, 3, 2).reshape(g * 512, n)
def pack4(w):
    words, scales = pack_weight(w, "e2m1")
    return words.reshape(words.shape[0], 128, -1), scales


def unpack4(words, scales):
    return unpack_weight(words.reshape(words.shape[0], 128, -1, 2), scales, "e2m1")


H, B, D, M = 4, 1024, 512, 1024


def setup_inputs():
    s = mx_kscale(H * D).reshape(H, 1, D)
    t = mx_kscale(H * M).reshape(H, M)
    bank = np.random.standard_normal((H, M, D)) / np.sqrt(D)
    kt = (bank / s).swapaxes(1, 2).reshape(H * D, M)
    kr = (bank / t[:, :, None]).reshape(H * M, D)
    kt_words, kt_scales = pack4(kt)
    kr_words, kr_scales = pack4(kr)
    return {"student": bf(np.random.standard_normal((H, B, D)) * s),
            "teacher": bf(np.random.standard_normal((H, B, M))),
            "anchor_w": bf(np.random.uniform(0.5, 1.5, (H, M)) * t),
            "kt_words": kt_words, "kt_scales": kt_scales,
            "kr_words": kr_words, "kr_scales": kr_scales}


def reference(student, teacher, anchor_w, kt_words, kt_scales, kr_words, kr_scales):
    kt = unpack4(kt_words, kt_scales).reshape(H, D, M)
    kr = unpack4(kr_words, kr_scales).reshape(H, M, D)
    gram = mxq(f64(student), 2, "e4m3") @ kt
    err = (gram - f64(teacher)) * f64(anchor_w)[:, None, :]
    grad = mxq(err, 2, "e4m3") @ kr
    return grad

from contextlib import ExitStack

import concourse.mybir as mybir
from concourse.masks import make_identity

H, B, D, M = 4, 1024, 512, 1024
FLOPS = 2 * 2 * H * B * D * M

F32 = mybir.dt.float32
BF16 = mybir.dt.bfloat16
I32 = mybir.dt.int32
U32 = mybir.dt.uint32
U8 = mybir.dt.uint8
FP8X4 = mybir.dt.float8_e4m3fn_x4
FP4X4 = mybir.dt.float4_e2m1fn_x4
ALU = mybir.AluOpType
COPY = mybir.ActivationFunctionType.Copy

P = 128
TILES = 2
ROWS = P * TILES
STEPS_PER_BAND = B // ROWS
STEPS = H * STEPS_PER_BAND
KP = 512
BANKS = 8
POOL_COLS = 832
OVERLAP = 16
LEAD = 3
BOTH_QUAD = ()
LAST = STEPS - 1


def tile_relational_distillation_gradient_s14_kernel(
    tc, student, teacher, anchor_w, kt_words, kt_scales, kr_words, kr_scales, out
):
    nc = tc.nc
    with ExitStack() as ctx:
        keep = ctx.enter_context(tc.tile_pool(name="keep", bufs=1))
        work = ctx.enter_context(tc.tile_pool(name="work", bufs=4))
        psum = ctx.enter_context(tc.psum_pool(name="psum", bufs=1))
        ctx.enter_context(tc.manual_schedule())

        bank_uses = []

        def next_bank():
            slot = len(bank_uses) % BANKS
            bank_uses.append(slot)
            return psum.tile([P, KP], F32, name="bank%d" % slot, tag="bank%d" % slot)

        def rows_of(tensor, k):
            h, s = divmod(k, STEPS_PER_BAND)
            return tensor[h, s * ROWS : (s + 1) * ROWS, :].rearrange("(p j) n -> p j n", j=TILES)

        ident = keep.tile([P, P], F32)
        kt_codes = keep.tile([P, H, 2 * M], U8, align_bytes=64)
        kt_plane = keep.tile([P, H, M], U8, align_bytes=64)
        kr_codes = keep.tile([P, 2 * H, 2 * D], U8, align_bytes=64)
        kr_plane = keep.tile([P, 2 * H, D], U8, align_bytes=64)
        w_rows = keep.tile([P, KP], BF16)
        w_part = keep.tile([P, 2 * H, 4], BF16)
        w_part32 = keep.tile([P, 2 * H, 4], F32)
        w_free = keep.tile([P, H, M], BF16)
        warm = keep.tile([P, 1], F32)
        warm_out = keep.tile([P, 1], F32)
        stu = [keep.tile([P, TILES, D], BF16, name="stu%d" % k) for k in range(STEPS)]
        tea = [keep.tile([P, TILES, M], BF16, name="tea%d" % k) for k in range(STEPS)]

        def load_student(k, j0=0, j1=TILES):
            nc.sync.dma_start(out=stu[k][:, j0:j1, :], in_=rows_of(student, k)[:, j0:j1, :])

        def load_teacher(k, j0=0, j1=TILES):
            nc.sync.dma_start(out=tea[k][:, j0:j1, :], in_=rows_of(teacher, k)[:, j0:j1, :])

        def load_kt_codes(h):
            nc.sync.dma_start(out=kt_codes[:, h, :].bitcast(I32), in_=kt_words[h].bitcast(I32))

        def load_kr_codes(h):
            nc.sync.dma_start(
                out=kr_codes[:, 2 * h : 2 * h + 2, :].bitcast(I32),
                in_=kr_words[2 * h : 2 * h + 2].bitcast(I32).rearrange("g p n -> p g n"),
            )

        def load_scales(plane, scales, g0, g1):
            for q in range(4):
                nc.sync.dma_start(
                    out=plane[32 * q : 32 * q + 4, g0:g1, :].bitcast(I32),
                    in_=scales[g0:g1, 4 * q : 4 * q + 4, :].bitcast(I32).rearrange("g r n -> r g n"),
                )

        make_identity(nc, ident[:])
        nc.vector.memset(w_rows[:].bitcast(F32), 0.0)
        nc.vector.memset(kt_plane[:, 0, :].bitcast(I32), 0)
        nc.vector.memset(warm[:], 0.0)
        nc.scalar.activation(out=warm_out[:], in_=warm[:], func=COPY)
        nc.vector.memset(kr_plane[:].rearrange("p h n -> p (h n)").bitcast(I32), 0)
        nc.vector.memset(kt_plane[:, 1:H, :].rearrange("p h n -> p (h n)").bitcast(I32), 0)

        load_student(0)
        nc.sync.dma_start(out=w_rows[0 : 2 * H, :], in_=anchor_w.rearrange("h (g n) -> (h g) n", g=2))
        load_kt_codes(0)
        load_scales(kt_plane, kt_scales, 0, 1)
        load_teacher(0, 0, 1)
        load_student(1)
        load_teacher(0, 1, 2)
        load_teacher(1)
        load_student(2)
        load_student(3)
        load_teacher(2)
        load_student(4)
        load_scales(kr_plane, kr_scales, 0, 2)
        load_kr_codes(0)
        load_student(5)

        s_grp, s_codes, s_plane = {}, {}, {}
        diff, err, flat, res = {}, {}, {}, {}
        e_grp, e_codes, e_plane = {}, {}, {}
        banks = {}

        def student_transposes(k, tiles=(0, 1)):
            banks["s", k, tiles[0]] = next_bank()
            for j in tiles:
                words = stu[k][:, j, :].bitcast(F32)
                for u in range(2):
                    c = (2 * j + u) * P
                    nc.tensor.transpose(banks["s", k, tiles[0]][:, c : c + P], words[:, u : 2 * P : 2], ident[:])

        def student_copy(k, tiles=(0, 1)):
            if tiles[0] == 0:
                s_grp[k] = work.tile([P, ROWS * 4], BF16, name="s_grp", bufs=LEAD + 1, align_bytes=64)
            c0, c1 = tiles[0] * 2 * P, (tiles[-1] + 1) * 2 * P
            nc.scalar.copy(
                out=s_grp[k][:].bitcast(F32)[:, c0:c1].rearrange("p (j b u) -> p j b u", b=P, u=2),
                in_=banks["s", k, tiles[0]][:, c0:c1].rearrange("p (j u b) -> p j b u", b=P, u=2),
            )

        def student_quantize(k, tiles=(0, 1)):
            if tiles[0] == 0:
                s_codes[k] = work.tile([P, ROWS], U32, name="s_codes", align_bytes=64)
                s_plane[k] = work.tile([P, ROWS], U8, name="s_plane", align_bytes=64)
            c0, c1 = tiles[0] * P, (tiles[-1] + 1) * P
            nc.vector.quantize_mx(
                out=s_codes[k][:, c0:c1].bitcast(FP8X4), scales=s_plane[k][:, c0:c1], in_=s_grp[k][:, 4 * c0 : 4 * c1]
            )

        def gram(k, parts):
            h = k // STEPS_PER_BAND
            for j, g in parts:
                bank = next_bank()
                nc.tensor.matmul_mx(
                    out=bank[:],
                    lhsT=s_codes[k][:, j * P : (j + 1) * P].bitcast(FP8X4),
                    lhsT_scale=s_plane[k][:, j * P : (j + 1) * P],
                    rhs=kt_codes[:, h, 2 * KP * g : 2 * KP * (g + 1)].bitcast(FP4X4),
                    rhs_scale=kt_plane[:, h, KP * g : KP * (g + 1)],
                    start=True,
                    stop=True,
                )
                banks["g", k, j, g] = bank

        def quad_groups(k):
            return (0, 1) if k in BOTH_QUAD else (1,)

        def subtract(k, parts):
            if k not in diff:
                diff[k] = work.tile([P, TILES * M], F32, name="diff")
            for j, g in parts:
                c = (2 * j + g) * KP
                if j == 1 and g in quad_groups(k):
                    dst, src, sizes = "b (t c i) -> b c t i", "b (c i t) -> b c t i", {"t": 4, "i": 4}
                else:
                    dst, src, sizes = "b (u q e) -> b q u e", "b (q u e) -> b q u e", {"u": 2, "e": 2}
                nc.vector.tensor_tensor(
                    out=diff[k][:, c : c + KP].rearrange(dst, **sizes),
                    in0=banks["g", k, j, g][:].rearrange(src, **sizes),
                    in1=tea[k][:, j, g * KP : (g + 1) * KP].rearrange(src, **sizes),
                    op=ALU.subtract,
                )

        def weigh(engine, k, c0, c1):
            h = k // STEPS_PER_BAND
            if k not in err:
                err[k] = work.tile([P, 3 * KP], BF16, name="err")
            w0 = c0 % M
            engine.tensor_tensor(
                out=err[k][:, c0:c1], in0=diff[k][:, c0:c1], in1=w_free[:, h, w0 : w0 + c1 - c0], op=ALU.mult
            )

        def weigh_rows(k):
            if k not in BOTH_QUAD:
                weigh(nc.vector, k, M, M + KP)
            weigh(nc.vector, k, POOL_COLS - OVERLAP, M)
            weigh(nc.gpsimd, k, 0, POOL_COLS)

        def quad_transposes(k):
            for g in quad_groups(k):
                bank = next_bank()
                for t in range(4):
                    c = M + g * KP + t * P
                    nc.tensor.transpose(bank[:, t * P : (t + 1) * P], diff[k][:, c : c + P], ident[:])
                banks["d", k, g] = bank

        def pair_transposes(k, j):
            count = 4 if j == 0 else 4 - 2 * len(quad_groups(k))
            if count:
                words = err[k][:].bitcast(F32)
                bank = next_bank()
                for c in range(count):
                    w0 = (4 * j + c) * P
                    nc.tensor.transpose(bank[:, c * P : (c + 1) * P], words[:, w0 : w0 + P], ident[:])
                banks["e", k, j] = bank

        def grouped(k):
            if k not in e_grp:
                e_grp[k] = work.tile([P, TILES * M], BF16, name="e_grp", align_bytes=64)
            return e_grp[k]

        def quad_scale(k):
            h = k // STEPS_PER_BAND
            flat[k] = work.tile([P, 2, 4, P], BF16, name="e_flat")
            for g in quad_groups(k):
                for t in range(4):
                    nc.scalar.activation(
                        out=flat[k][:, g, t, :],
                        in_=banks["d", k, g][:, t * P : (t + 1) * P],
                        func=COPY,
                        scale=w_part32[:, 2 * h + g, t : t + 1],
                    )

        def quad_interleave(k, copy):
            for g in quad_groups(k):
                c = M + g * KP
                copy(
                    out=grouped(k)[:, c : c + KP].rearrange("p (c i t) -> p c t i", i=4, t=4),
                    in_=flat[k][:, g, :, :].rearrange("p t (c i) -> p c t i", i=4),
                )

        def pair_copy(k, j, copy):
            if ("e", k, j) in banks:
                width = KP if j == 0 else KP // 2
                copy(
                    out=grouped(k)[:].bitcast(F32)[:, j * KP : j * KP + width].rearrange("p (g b u) -> p g b u", b=P, u=2),
                    in_=banks["e", k, j][:, 0:width].rearrange("p (g u b) -> p g b u", b=P, u=2),
                )

        def error_quantize(k, tiles=(0, 1)):
            if k not in e_codes:
                e_codes[k] = work.tile([P, 2 * ROWS], U32, name="e_codes", align_bytes=64)
                e_plane[k] = work.tile([P, 2 * ROWS], U8, name="e_plane", align_bytes=64)
            c0, c1 = tiles[0] * 2 * P, (tiles[-1] + 1) * 2 * P
            nc.vector.quantize_mx(
                out=e_codes[k][:, c0:c1].bitcast(FP8X4), scales=e_plane[k][:, c0:c1], in_=e_grp[k][:, 4 * c0 : 4 * c1]
            )

        def gradient(k, tiles=(0, 1)):
            h = k // STEPS_PER_BAND
            for j in tiles:
                bank = next_bank()
                for g in range(2):
                    c = (2 * j + g) * P
                    nc.tensor.matmul_mx(
                        out=bank[:],
                        lhsT=e_codes[k][:, c : c + P].bitcast(FP8X4),
                        lhsT_scale=e_plane[k][:, c : c + P],
                        rhs=kr_codes[:, 2 * h + g, :].bitcast(FP4X4),
                        rhs_scale=kr_plane[:, 2 * h + g, :],
                        start=(g == 0),
                        stop=(g == 1),
                    )
                banks["o", k, j] = bank

        def result_copy(k, j, copy):
            if k not in res:
                res[k] = work.tile([P, TILES, D], F32, name="res")
            copy(out=res[k][:, j, :], in_=banks["o", k, j][:])

        def store(k, j0=0, j1=TILES):
            nc.sync.dma_start(out=rows_of(out, k)[:, j0:j1, :], in_=res[k][:, j0:j1, :])

        def weights_to_partitions():
            bank = next_bank()
            words = w_rows[:].bitcast(F32)
            for u in range(2):
                nc.tensor.transpose(bank[:, u * P : (u + 1) * P], words[:, u : 2 * P : 2], ident[:])
            nc.scalar.copy(
                out=w_part[:].rearrange("p r t -> p (r t)").bitcast(F32).rearrange("p (r u) -> p r u", u=2),
                in_=bank[:, 0 : 2 * P].rearrange("p (u r) -> p r u", u=2)[:, 0 : 2 * H, :],
            )
            nc.scalar.copy(out=w_part32[:], in_=w_part[:])

        def weights_to_rows(h):
            words = w_part[:].rearrange("p r t -> p (r t)").bitcast(F32)
            bank = next_bank()
            for c in range(4):
                col = 4 * h + c
                nc.tensor.transpose(bank[:, c * P : (c + 1) * P], words[:, col : col + 1].to_broadcast([P, P]), ident[:])
            nc.scalar.copy(out=w_free[:, h, :].bitcast(F32), in_=bank[:])

        act, dve = nc.scalar.copy, nc.vector.tensor_copy
        parts = [(0, 0), (0, 1), (1, 0), (1, 1)]
        last_parts = [(1, 1), (1, 0), (0, 0), (0, 1)]

        for j in range(TILES):
            student_transposes(0, (j,))
            student_copy(0, (j,))
            student_quantize(0, (j,))
        weights_to_partitions()
        gram(0, parts[0:2])
        student_transposes(1)
        student_copy(1)
        gram(0, parts[2:4])
        weights_to_rows(0)
        subtract(0, parts[0:3])
        student_quantize(1)
        subtract(0, parts[3:4])
        gram(1, parts)

        for n in range(STEPS):
            if n > 0:
                subtract(n, parts if n < LAST else last_parts)
            for k in range(2, LEAD) if n == 0 else []:
                student_transposes(k)
                student_copy(k)
            if n + LEAD < STEPS:
                student_transposes(n + LEAD)
                student_copy(n + LEAD)
            if n in (1, 2, 3):
                weights_to_rows(n)
            if n >= 1:
                quad_transposes(n - 1)
                pair_transposes(n - 1, 0)
                pair_transposes(n - 1, 1)
                quad_scale(n - 1)
                pair_copy(n - 1, 0, act)
                pair_copy(n - 1, 1, act)
                quad_interleave(n - 1, act)
            if n == 0:
                weigh_rows(0)
            if n == 1:
                student_quantize(2)
            if 1 <= n < STEPS - 2:
                student_quantize(n + 2)
            if n >= 2:
                error_quantize(n - 2)
            if 0 < n < LAST:
                gram(n + 1, parts if n + 1 < LAST else last_parts)
                weigh_rows(n)
            if n + LEAD + 2 < STEPS:
                load_student(n + LEAD + 2)
            if n + 3 < STEPS:
                load_teacher(n + 3)
            if n == 0:
                load_scales(kt_plane, kt_scales, 1, H)
                load_scales(kr_plane, kr_scales, 2, 2 * H)
            if n < H - 1:
                load_kt_codes(n + 1)
            if 1 <= n < H:
                load_kr_codes(n)
            if 2 <= n < LAST:
                gradient(n - 2)
                result_copy(n - 2, 0, act)
                result_copy(n - 2, 1, act)
                store(n - 2)

        k = LAST
        quad_transposes(k)
        gradient(k - 2)
        weigh(nc.vector, k, M, M + KP)
        weigh(nc.vector, k, 0, M)
        quad_scale(k)
        pair_transposes(k, 1)
        pair_transposes(k, 0)
        error_quantize(k - 1)
        result_copy(k - 2, 0, act)
        result_copy(k - 2, 1, act)
        store(k - 2)
        gradient(k - 1)
        pair_copy(k, 1, dve)
        quad_interleave(k, dve)
        pair_copy(k, 0, dve)
        error_quantize(k, (1,))
        error_quantize(k, (0,))
        result_copy(k - 1, 0, act)
        result_copy(k - 1, 1, act)
        store(k - 1)
        gradient(k, (1, 0))
        result_copy(k, 1, dve)
        store(k, 1, 2)
        result_copy(k, 0, act)
        store(k, 0, 1)
